import numpy as np
import ml_dtypes


def mxq(x, axis, fmt="e4m3"):
    dtype, down = {"e4m3": (ml_dtypes.float8_e4m3fn, 7), "e5m2": (ml_dtypes.float8_e5m2, 14)}[fmt]
    v = np.moveaxis(np.asarray(x, np.float32).astype(ml_dtypes.bfloat16).astype(np.float64), axis, -1)
    blocks = v.reshape(v.shape[:-1] + (-1, 32))
    amax = np.abs(blocks).max(-1, keepdims=True)
    byte = np.maximum(np.where(amax > 0, np.frexp(amax)[1] - 1 + 127, 0) - down, 1)
    scale = np.exp2(byte - 127.0)
    codes = (blocks / scale).astype(np.float32).astype(dtype).astype(np.float64)
    return np.moveaxis((codes * scale).reshape(v.shape), -1, axis)


WIDE = False


def mx_kscale(k):
    if not WIDE:
        return np.ones(k)
    levels = np.array([10, -10, 5, -5, 0])
    if k % 512:
        return np.exp2(np.random.permutation(np.resize(levels, k // 32))).repeat(32)
    a = np.empty((k // 512, 16))
    for p in range(k // 512):
        a[p, :8] = np.random.permutation(np.resize(levels, 8))
        for g in range(8):
            far = levels[np.abs(levels - a[p, g]) >= 10]
            a[p, g + 8] = far[np.random.randint(len(far))]
    return np.exp2(a.ravel()).repeat(32)


BF16 = ml_dtypes.bfloat16


def bf(x):
    return np.asarray(x, np.float32).astype(BF16)


def f64(x):
    return np.asarray(x).astype(np.float64)


E2M1 = np.array([0.0, 0.5, 1.0, 1.5, 2.0, 3.0, 4.0, 6.0, -0.0, -0.5, -1.0, -1.5, -2.0, -3.0, -4.0, -6.0])


def pack_weight(w, fmt):
    k, n = w.shape
    w = f64(bf(w)).reshape(k // 32, 32, n)
    amax = np.abs(w).max(1)
    if fmt == "e4m3":
        byte = np.frexp(amax)[1] - 1 + 127 - 7
    else:
        mant, ex = np.frexp(amax / 6.0)
        byte = np.where(mant > 0.5, ex, ex - 1) + 127
    byte = np.clip(np.where(amax > 0, byte, 1), 1, 254)
    scaled = (w * np.exp2(127.0 - byte)[:, None, :]).reshape(k, n).astype(np.float32)
    by_word = np.ascontiguousarray(scaled.reshape(k // 512, 128, 4, n).transpose(0, 1, 3, 2))
    if fmt == "e4m3":
        words = by_word.astype(ml_dtypes.float8_e4m3fn).view(np.uint8)
    else:
        c = by_word.astype(ml_dtypes.float4_e2m1fn).view(np.uint8) & 0xF
        words = c[..., 0::2] | (c[..., 1::2] << 4)
    return np.ascontiguousarray(words), np.ascontiguousarray(byte.astype(np.uint8).reshape(k // 512, 16, n))


def unpack_weight(words, scales, fmt):
    g, p, n, _ = words.shape
    if fmt == "e4m3":
        vals = np.ascontiguousarray(words).view(ml_dtypes.float8_e4m3fn).astype(np.float64)
    else:
        nib = np.empty((g, p, n, 4), np.uint8)
        nib[..., 0::2] = words & 0xF
        nib[..., 1::2] = words >> 4
        vals = E2M1[nib]
    vals = vals * np.repeat(np.exp2(scales.astype(np.float64) - 127.0), 8, axis=1)[..., None]
    return vals.transpose(0, 1, 3, 2).reshape(g * 512, n)
def pack4(w):
    words, scales = pack_weight(w, "e2m1")
    return words.reshape(words.shape[0], 128, -1), scales


def unpack4(words, scales):
    return unpack_weight(words.reshape(words.shape[0], 128, -1, 2), scales, "e2m1")


M, K, N = 512, 2048, 1536


def setup_inputs():
    s = mx_kscale(K)
    path = np.random.standard_normal((K, N)) * 2.0 / np.sqrt(K) / s[:, None]
    leaf = np.random.standard_normal((K, N)) * 1.4 / np.sqrt(K) / s[:, None]
    corr = np.random.standard_normal((K, N)) / np.sqrt(K) / s[:, None]
    path_words, path_scales = pack4(path)
    leaf_words, leaf_scales = pack_weight(leaf, "e4m3")
    return {"x": bf(np.random.standard_normal((M, K))),
            "thr": bf(0.5 * np.random.standard_normal(K)),
            "gain": bf((1.0 + 0.1 * np.random.standard_normal(K)) * s),
            "path_words": path_words, "path_scales": path_scales,
            "count": bf(0.5 * np.random.standard_normal(N)),
            "leaf_words": leaf_words, "leaf_scales": leaf_scales,
            "corr": bf(corr)}


def reference(x, thr, gain, path_words, path_scales, count, leaf_words, leaf_scales, corr):
    d = (f64(x) > f64(thr)) * f64(gain)
    a = mxq(d, 1, "e4m3")
    hits = a @ unpack4(path_words, path_scales)
    value = a @ unpack_weight(leaf_words, leaf_scales, "e4m3")
    extra = a @ mxq(f64(corr), 0, "e4m3")
    reach = 1.0 / (1.0 + np.exp(-(hits - f64(count))))
    return reach * value + extra

@@ -1,0 +1,319 @@
+from contextlib import ExitStack
+
+import concourse.mybir as mybir
+from concourse.masks import make_identity
+
+M, K, N = 512, 2048, 1536
+FLOPS = 3 * 2 * M * K * N
+
+F32 = mybir.dt.float32
+BF16 = mybir.dt.bfloat16
+I32 = mybir.dt.int32
+U32 = mybir.dt.uint32
+U8 = mybir.dt.uint8
+FP8X4 = mybir.dt.float8_e4m3fn_x4
+FP4X4 = mybir.dt.float4_e2m1fn_x4
+ALU = mybir.AluOpType
+ACT = mybir.ActivationFunctionType
+
+P = 128
+PACK = 4
+K_PASS = P * PACK
+PASSES = K // K_PASS
+N_TILE = 512
+M_TILES = M // P
+N_TILES = N // N_TILE
+TILES = M_TILES * N_TILES
+CHUNKS = N_TILES * PASSES
+BANKS = 8
+SCALAR_COLS = 384
+COUNT_BLOCKS = N // 2 // P
+
+
+def tile_tree_path_leaf_response_s10_kernel(
+    tc, x, thr, gain, path_words, path_scales, count, leaf_words, leaf_scales, corr, out
+):
+    nc = tc.nc
+    with ExitStack() as ctx:
+        keep = ctx.enter_context(tc.tile_pool(name="keep", bufs=1))
+        stage = ctx.enter_context(tc.tile_pool(name="stage", bufs=3))
+        psum = ctx.enter_context(tc.psum_pool(name="psum", bufs=1))
+        ctx.enter_context(tc.manual_schedule())
+
+        def bank_tile(b):
+            return psum.tile([P, N_TILE], F32, name="bank%d" % b)
+
+        ident = keep.tile([P, P], F32, name="ident")
+        make_identity(nc, ident[:])
+
+        thr_sb = keep.tile([P, PASSES, PACK], BF16, name="thr_sb")
+        gain_sb = keep.tile([P, PASSES, PACK], BF16, name="gain_sb")
+        count_words = keep.tile([P, COUNT_BLOCKS], F32, name="count_words")
+        nc.scalar.dma_start(out=thr_sb[:], in_=thr.rearrange("(g p t) -> p g t", p=P, t=PACK))
+        nc.scalar.dma_start(out=gain_sb[:], in_=gain.rearrange("(g p t) -> p g t", p=P, t=PACK))
+        with nc.allow_non_contiguous_dma(reason="one word of count to a partition"):
+            nc.scalar.dma_start(out=count_words[:], in_=count.bitcast(F32).rearrange("(c p) -> p c", p=P))
+
+        path_sc_first = keep.tile([P, PASSES, N_TILE], U8, name="path_sc_first", align_bytes=64)
+        path_sc_rest = keep.tile([P, PASSES, N - N_TILE], U8, name="path_sc_rest", align_bytes=64)
+        leaf_sc = keep.tile([P, N], U8, name="leaf_sc", align_bytes=64)
+        nc.vector.memset(path_sc_first[:].rearrange("p g n -> p (g n)").bitcast(I32), 0)
+        nc.vector.memset(leaf_sc[:].bitcast(I32), 0)
+        nc.vector.memset(path_sc_rest[:].rearrange("p g n -> p (g n)").bitcast(I32), 0)
+
+        x_sb = {}
+        path_sb = {}
+        leaf_sb = {}
+        corr_sb = {}
+
+        def load_x(m, h0, h1):
+            t = keep.tile([P, (h1 - h0) * 2 * K_PASS], BF16, name="x%d_%d" % (m, h0))
+            nc.sync.dma_start(out=t[:], in_=x[m * P : (m + 1) * P, h0 * 2 * K_PASS : h1 * 2 * K_PASS])
+            for h in range(h0, h1):
+                x_sb[m, h] = t[:, (h - h0) * 2 * K_PASS : (h - h0 + 1) * 2 * K_PASS]
+
+        def load_path(n):
+            t = keep.tile([P, PASSES, 2 * N_TILE], U8, name="path%d" % n, align_bytes=64)
+            src = path_words[:, :, n * 2 * N_TILE : (n + 1) * 2 * N_TILE].rearrange("g p b -> p g b")
+            nc.sync.dma_start(out=t[:].bitcast(I32), in_=src.bitcast(I32))
+            path_sb[n] = t
+
+        def load_leaf(n):
+            t = keep.tile([P, PASSES, N_TILE], U32, name="leaf%d" % n, align_bytes=64)
+            src = leaf_words.rearrange("g p n t -> p g (n t)")[:, :, n * 4 * N_TILE : (n + 1) * 4 * N_TILE]
+            nc.sync.dma_start(out=t[:].bitcast(I32), in_=src.bitcast(I32))
+            leaf_sb[n] = t
+
+        def load_path_scales(plane, n0, n1):
+            for q in range(4):
+                src = path_scales[:, 4 * q : 4 * q + 4, n0:n1].rearrange("g r n -> r g n")
+                nc.sync.dma_start(out=plane[32 * q : 32 * q + 4, :, :].bitcast(I32), in_=src.bitcast(I32))
+
+        def load_leaf_scales():
+            for q in range(4):
+                nc.sync.dma_start(
+                    out=leaf_sc[32 * q : 32 * q + 16, :].bitcast(I32),
+                    in_=leaf_scales[:, 4 * q : 4 * q + 4, :].bitcast(I32),
+                )
+
+        def load_corr(c):
+            n, g = divmod(c, PASSES)
+            t = keep.tile([P, PACK, N_TILE], BF16, name="corr%d" % c)
+            src = corr[g * K_PASS : (g + 1) * K_PASS, n * N_TILE : (n + 1) * N_TILE]
+            nc.sync.dma_start(out=t[:], in_=src.rearrange("(p t) n -> p t n", t=PACK))
+            corr_sb[c] = t
+
+        load_x(0, 0, 1)
+        load_x(0, 1, 2)
+        for m in range(1, M_TILES):
+            load_x(m, 0, 2)
+        load_path(0)
+        load_path_scales(path_sc_first, 0, N_TILE)
+        load_leaf(0)
+        load_leaf_scales()
+        load_corr(0)
+        load_path(1)
+        load_path_scales(path_sc_rest, N_TILE, N)
+        load_corr(1)
+        load_leaf(1)
+        for c in (2, 3, 4):
+            load_corr(c)
+        load_path(2)
+        load_leaf(2)
+        for c in range(5, CHUNKS):
+            load_corr(c)
+
+        xt = {}
+
+        def transpose_x(m, h):
+            bank = bank_tile(2 * m + h)
+            words = x_sb[m, h].bitcast(F32)
+            for gg in range(2):
+                for u in range(2):
+                    col = (2 * u + gg) * P
+                    nc.tensor.transpose(
+                        bank[:, col : col + P], words[:, 256 * gg + u : 256 * (gg + 1) : 2], ident[:]
+                    )
+            xt[m, h] = bank
+
+        count_all = keep.tile([P, N], BF16, name="count_all")
+
+        def spread_count():
+            for b0 in range(0, COUNT_BLOCKS, 4):
+                nb = min(4, COUNT_BLOCKS - b0)
+                bank = bank_tile(BANKS - 2 + b0 // 4)
+                for c in range(nb):
+                    nc.tensor.transpose(
+                        bank[:, c * P : (c + 1) * P],
+                        count_words[:, b0 + c : b0 + c + 1].to_broadcast([P, P]),
+                        ident[:],
+                    )
+                nc.scalar.copy(out=count_all[:].bitcast(F32)[:, b0 * P : (b0 + nb) * P], in_=bank[:, : nb * P])
+
+        transpose_x(0, 0)
+        transpose_x(0, 1)
+        spread_count()
+        for m in range(1, M_TILES):
+            transpose_x(m, 0)
+            transpose_x(m, 1)
+
+        d_bf = {}
+        d_codes = {}
+        d_scales = {}
+
+        def compare(m, h):
+            t = stage.tile([P, 2 * K_PASS], BF16, name="d_bf", align_bytes=64, bufs=4)
+            shape = [P, 2, P, 2, 2]
+            nc.vector.tensor_tensor(
+                out=t[:].rearrange("p (g m u e) -> p g m u e", g=2, u=2, e=2),
+                in0=xt[m, h][:].bitcast(BF16).rearrange("p (u g m e) -> p g m u e", u=2, g=2, e=2),
+                in1=thr_sb[:, 2 * h : 2 * h + 2, :].rearrange("p g (u e) -> p g u e", e=2).unsqueeze(2).to_broadcast(shape),
+                op=ALU.is_gt,
+            )
+            d_bf[m, h] = t
+
+        def weight(m, h):
+            view = d_bf[m, h][:].rearrange("p (g m t) -> p g m t", g=2, t=PACK)
+            nc.vector.tensor_tensor(
+                out=view,
+                in0=view,
+                in1=gain_sb[:, 2 * h : 2 * h + 2, :].unsqueeze(2).to_broadcast([P, 2, P, PACK]),
+                op=ALU.mult,
+            )
+
+        def quantize_d(m, h):
+            codes = keep.tile([P, 2 * P], U32, name="d_codes%d_%d" % (m, h), align_bytes=64)
+            scales = keep.tile([P, 2 * P], U8, name="d_scales%d_%d" % (m, h), align_bytes=64)
+            nc.vector.quantize_mx(out=codes[:].bitcast(FP8X4), scales=scales[:], in_=d_bf[m, h][:])
+            for gg in range(2):
+                d_codes[m, 2 * h + gg] = codes[:, gg * P : (gg + 1) * P]
+                d_scales[m, 2 * h + gg] = scales[:, gg * P : (gg + 1) * P]
+
+        groups = []
+
+        def product(m, rhs_of_pass):
+            bank = bank_tile(len(groups) % BANKS)
+            groups.append(bank)
+            for g in range(PASSES):
+                rhs, rhs_scale = rhs_of_pass(g)
+                nc.tensor.matmul_mx(
+                    out=bank[:],
+                    lhsT=d_codes[m, g].bitcast(FP8X4),
+                    lhsT_scale=d_scales[m, g],
+                    rhs=rhs,
+                    rhs_scale=rhs_scale,
+                    start=(g == 0),
+                    stop=(g == PASSES - 1),
+                )
+            return bank
+
+        hits = {}
+        value = {}
+        extra = {}
+        corr_bf = {}
+        corr_codes = {}
+        corr_scales = {}
+        reach = {}
+        result = {}
+
+        def cols(n):
+            return slice(n * N_TILE, (n + 1) * N_TILE)
+
+        def hits_product(i):
+            n, m = divmod(i, M_TILES)
+            plane = path_sc_first if n == 0 else path_sc_rest
+            n_in = 0 if n == 0 else n - 1
+            hits[i] = product(m, lambda g: (path_sb[n][:, g, :].bitcast(FP4X4), plane[:, g, cols(n_in)]))
+
+        def value_product(i):
+            n, m = divmod(i, M_TILES)
+            value[i] = product(m, lambda g: (leaf_sb[n][:, g, :].bitcast(FP8X4), leaf_sc[4 * g :, cols(n)]))
+
+        def extra_product(i):
+            n, m = divmod(i, M_TILES)
+            extra[i] = product(
+                m, lambda g: (corr_codes[n * PASSES + g][:].bitcast(FP8X4), corr_scales[n * PASSES + g][:])
+            )
+
+        def interleave_views(c, c0, c1):
+            dst = corr_bf[c][:, c0 * PACK : c1 * PACK].rearrange("p (c i t) -> p c t i", i=4, t=PACK)
+            src = corr_sb[c][:, :, c0:c1].rearrange("p t (c i) -> p c t i", i=4)
+            return dst, src
+
+        def interleave_scalar(c):
+            corr_bf[c] = stage.tile([P, N_TILE * PACK], BF16, name="corr_bf", align_bytes=64, bufs=3)
+            dst, src = interleave_views(c, 0, SCALAR_COLS)
+            nc.scalar.copy(out=dst, in_=src)
+
+        def interleave_vector(c):
+            dst, src = interleave_views(c, SCALAR_COLS, N_TILE)
+            nc.vector.tensor_copy(out=dst, in_=src)
+
+        def quantize_corr(c):
+            corr_codes[c] = keep.tile([P, N_TILE], U32, name="corr_codes%d" % c, align_bytes=64)
+            corr_scales[c] = keep.tile([P, N_TILE], U8, name="corr_scales%d" % c, align_bytes=64)
+            nc.vector.quantize_mx(out=corr_codes[c][:].bitcast(FP8X4), scales=corr_scales[c][:], in_=corr_bf[c][:])
+
+        def subtract_count(i):
+            reach[i] = stage.tile([P, N_TILE], F32, name="reach", bufs=4)
+            nc.vector.tensor_tensor(out=reach[i][:], in0=hits[i][:], in1=count_all[:, cols(i // M_TILES)], op=ALU.subtract)
+
+        def sigmoid(i):
+            nc.scalar.activation(out=reach[i][:], in_=reach[i][:], func=ACT.Sigmoid)
+
+        def gate_value(i):
+            result[i] = keep.tile([P, N_TILE], F32, name="result%d" % i)
+            nc.vector.tensor_tensor(out=result[i][:], in0=value[i][:], in1=reach[i][:], op=ALU.mult)
+
+        def add_extra(i):
+            n, m = divmod(i, M_TILES)
+            nc.vector.tensor_tensor(out=result[i][:], in0=extra[i][:], in1=result[i][:], op=ALU.add)
+            nc.sync.dma_start(out=out[m * P : (m + 1) * P, cols(n)], in_=result[i][:])
+
+        compare(0, 0)
+        for m in range(M_TILES):
+            compare(m, 1)
+            weight(m, 0)
+            weight(m, 1)
+            quantize_d(m, 0)
+            if m + 1 < M_TILES:
+                compare(m + 1, 0)
+                quantize_d(m, 1)
+
+        hits_product(0)
+        hits_product(1)
+        value_product(0)
+        value_product(1)
+        hits_product(2)
+        value_product(2)
+        interleave_scalar(0)
+
+        for i in range(TILES):
+            if i >= M_TILES - 1:
+                hits_product(i)
+                value_product(i)
+            subtract_count(i)
+            if i == 0:
+                quantize_d(M_TILES - 1, 1)
+            if i >= 3:
+                interleave_vector(i - 3)
+            if i >= 1:
+                gate_value(i - 1)
+            if i >= 3:
+                quantize_corr(i - 3)
+            sigmoid(i)
+            if i >= 2:
+                interleave_scalar(i - 1)
+        last = TILES - 1
+        for i in range(TILES):
+            extra_product(i)
+            late = CHUNKS - 3 + i // 2
+            if i % 2 == 1 and late < CHUNKS:
+                interleave_vector(late)
+            add_extra(i)
+            if i == 1:
+                gate_value(last)
+            if i % 2 == 1 and late < CHUNKS:
+                quantize_corr(late)
+            if i == 1:
+                interleave_scalar(CHUNKS - 1)

@@ -26,8 +26,11 @@ N_TILES = N // N_TILE
 TILES = M_TILES * N_TILES
 CHUNKS = N_TILES * PASSES
 BANKS = 8
-SCALAR_COLS = 384
-COUNT_BLOCKS = N // 2 // P
+SCALAR_COLS = 416
+GATE_LAG = 4
+QUANT_LAG = 6
+THR_ROW, GAIN_ROW, COUNT_ROW = 0, PASSES, 2 * PASSES
+VEC_ROWS = COUNT_ROW + N_TILES
 
 
 def tile_tree_path_leaf_response_s10_kernel(
@@ -43,23 +46,25 @@ def tile_tree_path_leaf_response_s10_kernel(
         def bank_tile(b):
             return psum.tile([P, N_TILE], F32, name="bank%d" % b)
 
+        vec_rows = keep.tile([P, K_PASS], BF16, name="vec_rows")
+        nc.gpsimd.memset(vec_rows[:].bitcast(I32), 0)
         ident = keep.tile([P, P], F32, name="ident")
         make_identity(nc, ident[:])
 
-        thr_sb = keep.tile([P, PASSES, PACK], BF16, name="thr_sb")
-        gain_sb = keep.tile([P, PASSES, PACK], BF16, name="gain_sb")
-        count_words = keep.tile([P, COUNT_BLOCKS], F32, name="count_words")
-        nc.scalar.dma_start(out=thr_sb[:], in_=thr.rearrange("(g p t) -> p g t", p=P, t=PACK))
-        nc.scalar.dma_start(out=gain_sb[:], in_=gain.rearrange("(g p t) -> p g t", p=P, t=PACK))
-        with nc.allow_non_contiguous_dma(reason="one word of count to a partition"):
-            nc.scalar.dma_start(out=count_words[:], in_=count.bitcast(F32).rearrange("(c p) -> p c", p=P))
+        def load_vectors():
+            count_rows = count.rearrange("(r k) -> r k", k=K_PASS)
+            nc.sync.dma_start(out=vec_rows[THR_ROW:GAIN_ROW, :], in_=thr.rearrange("(r k) -> r k", k=K_PASS))
+            nc.sync.dma_start(out=vec_rows[GAIN_ROW:COUNT_ROW, :], in_=gain.rearrange("(r k) -> r k", k=K_PASS))
+            nc.sync.dma_start(out=vec_rows[COUNT_ROW : COUNT_ROW + 2, :], in_=count_rows[:2, :])
+            nc.sync.dma_start(out=vec_rows[COUNT_ROW + 2 : VEC_ROWS, :], in_=count_rows[2:, :])
 
-        path_sc_first = keep.tile([P, PASSES, N_TILE], U8, name="path_sc_first", align_bytes=64)
-        path_sc_rest = keep.tile([P, PASSES, N - N_TILE], U8, name="path_sc_rest", align_bytes=64)
+        path_sc = {}
+        for n in range(N_TILES):
+            path_sc[n] = keep.tile([P, PASSES, N_TILE], U8, name="path_sc%d" % n, align_bytes=64)
         leaf_sc = keep.tile([P, N], U8, name="leaf_sc", align_bytes=64)
-        nc.vector.memset(path_sc_first[:].rearrange("p g n -> p (g n)").bitcast(I32), 0)
         nc.vector.memset(leaf_sc[:].bitcast(I32), 0)
-        nc.vector.memset(path_sc_rest[:].rearrange("p g n -> p (g n)").bitcast(I32), 0)
+        for n in range(N_TILES):
+            nc.vector.memset(path_sc[n][:].rearrange("p g n -> p (g n)").bitcast(I32), 0)
 
         x_sb = {}
         path_sb = {}
@@ -77,17 +82,15 @@ def tile_tree_path_leaf_response_s10_kernel(
             src = path_words[:, :, n * 2 * N_TILE : (n + 1) * 2 * N_TILE].rearrange("g p b -> p g b")
             nc.sync.dma_start(out=t[:].bitcast(I32), in_=src.bitcast(I32))
             path_sb[n] = t
+            for q in range(4):
+                rows = path_scales[:, 4 * q : 4 * q + 4, n * N_TILE : (n + 1) * N_TILE].rearrange("g r n -> r g n")
+                nc.sync.dma_start(out=path_sc[n][32 * q : 32 * q + 4, :, :].bitcast(I32), in_=rows.bitcast(I32))
 
         def load_leaf(n):
             t = keep.tile([P, PASSES, N_TILE], U32, name="leaf%d" % n, align_bytes=64)
             src = leaf_words.rearrange("g p n t -> p g (n t)")[:, :, n * 4 * N_TILE : (n + 1) * 4 * N_TILE]
             nc.sync.dma_start(out=t[:].bitcast(I32), in_=src.bitcast(I32))
             leaf_sb[n] = t
-
-        def load_path_scales(plane, n0, n1):
-            for q in range(4):
-                src = path_scales[:, 4 * q : 4 * q + 4, n0:n1].rearrange("g r n -> r g n")
-                nc.sync.dma_start(out=plane[32 * q : 32 * q + 4, :, :].bitcast(I32), in_=src.bitcast(I32))
 
         def load_leaf_scales():
             for q in range(4):
@@ -104,23 +107,22 @@ def tile_tree_path_leaf_response_s10_kernel(
             corr_sb[c] = t
 
         load_x(0, 0, 1)
+        load_vectors()
         load_x(0, 1, 2)
         for m in range(1, M_TILES):
             load_x(m, 0, 2)
         load_path(0)
-        load_path_scales(path_sc_first, 0, N_TILE)
         load_leaf(0)
         load_leaf_scales()
         load_corr(0)
         load_path(1)
-        load_path_scales(path_sc_rest, N_TILE, N)
         load_corr(1)
         load_leaf(1)
-        for c in (2, 3, 4):
+        for c in range(2, 7):
             load_corr(c)
         load_path(2)
         load_leaf(2)
-        for c in range(5, CHUNKS):
+        for c in range(7, CHUNKS):
             load_corr(c)
 
         xt = {}
@@ -138,19 +140,36 @@ def tile_tree_path_leaf_response_s10_kernel(
 
         count_all = keep.tile([P, N], BF16, name="count_all")
 
+        vec_cols = keep.tile([P, VEC_ROWS, 2], F32, name="vec_cols")
+        vec_bf = vec_cols[:].bitcast(BF16)
+
+        def transpose_vectors():
+            bank = bank_tile(BANKS - 3)
+            words = vec_rows[:].bitcast(F32)
+            for u in range(2):
+                nc.tensor.transpose(bank[:, u * P : (u + 1) * P], words[:, u::2], ident[:])
+            src = bank[:, : 2 * P].rearrange("p (u r) -> p r u", u=2)
+            nc.vector.tensor_copy(out=vec_cols[:], in_=src[:, :VEC_ROWS, :])
+
         def spread_count():
-            for b0 in range(0, COUNT_BLOCKS, 4):
-                nb = min(4, COUNT_BLOCKS - b0)
-                bank = bank_tile(BANKS - 2 + b0 // 4)
-                for c in range(nb):
-                    nc.tensor.transpose(
-                        bank[:, c * P : (c + 1) * P],
-                        count_words[:, b0 + c : b0 + c + 1].to_broadcast([P, P]),
-                        ident[:],
+            for n0 in range(0, N_TILES, 2):
+                bank = bank_tile(BANKS - 2 + n0 // 2)
+                tiles = range(n0, min(n0 + 2, N_TILES))
+                for n in tiles:
+                    for u in range(2):
+                        col = (2 * (n - n0) + u) * P
+                        column = vec_cols[:, COUNT_ROW + n, u : u + 1]
+                        nc.tensor.transpose(bank[:, col : col + P], column.to_broadcast([P, P]), ident[:])
+                for n in tiles:
+                    pairs = bank[:, (n - n0) * 2 * P : (n - n0 + 1) * 2 * P].bitcast(BF16)
+                    nc.scalar.activation(
+                        out=count_all[:, n * N_TILE : (n + 1) * N_TILE].rearrange("q (p u e) -> q p u e", u=2, e=2),
+                        in_=pairs.rearrange("q (u p e) -> q p u e", u=2, e=2),
+                        func=ACT.Copy,
                     )
-                nc.scalar.copy(out=count_all[:].bitcast(F32)[:, b0 * P : (b0 + nb) * P], in_=bank[:, : nb * P])
 
         transpose_x(0, 0)
+        transpose_vectors()
         transpose_x(0, 1)
         spread_count()
         for m in range(1, M_TILES):
@@ -167,7 +186,7 @@ def tile_tree_path_leaf_response_s10_kernel(
             nc.vector.tensor_tensor(
                 out=t[:].rearrange("p (g m u e) -> p g m u e", g=2, u=2, e=2),
                 in0=xt[m, h][:].bitcast(BF16).rearrange("p (u g m e) -> p g m u e", u=2, g=2, e=2),
-                in1=thr_sb[:, 2 * h : 2 * h + 2, :].rearrange("p g (u e) -> p g u e", e=2).unsqueeze(2).to_broadcast(shape),
+                in1=vec_bf[:, THR_ROW + 2 * h : THR_ROW + 2 * h + 2, :].rearrange("p g (u e) -> p g u e", e=2).unsqueeze(2).to_broadcast(shape),
                 op=ALU.is_gt,
             )
             d_bf[m, h] = t
@@ -177,7 +196,7 @@ def tile_tree_path_leaf_response_s10_kernel(
             nc.vector.tensor_tensor(
                 out=view,
                 in0=view,
-                in1=gain_sb[:, 2 * h : 2 * h + 2, :].unsqueeze(2).to_broadcast([P, 2, P, PACK]),
+                in1=vec_bf[:, GAIN_ROW + 2 * h : GAIN_ROW + 2 * h + 2, :].unsqueeze(2).to_broadcast([P, 2, P, PACK]),
                 op=ALU.mult,
             )
 
@@ -191,13 +210,13 @@ def tile_tree_path_leaf_response_s10_kernel(
 
         groups = []
 
-        def product(m, rhs_of_pass):
+        def product(m, rhs_of_pass, width=N_TILE):
             bank = bank_tile(len(groups) % BANKS)
             groups.append(bank)
             for g in range(PASSES):
                 rhs, rhs_scale = rhs_of_pass(g)
                 nc.tensor.matmul_mx(
-                    out=bank[:],
+                    out=bank[:, :width],
                     lhsT=d_codes[m, g].bitcast(FP8X4),
                     lhsT_scale=d_scales[m, g],
                     rhs=rhs,
@@ -205,7 +224,7 @@ def tile_tree_path_leaf_response_s10_kernel(
                     start=(g == 0),
                     stop=(g == PASSES - 1),
                 )
-            return bank
+            return bank[:, :width]
 
         hits = {}
         value = {}
@@ -221,18 +240,19 @@ def tile_tree_path_leaf_response_s10_kernel(
 
         def hits_product(i):
             n, m = divmod(i, M_TILES)
-            plane = path_sc_first if n == 0 else path_sc_rest
-            n_in = 0 if n == 0 else n - 1
-            hits[i] = product(m, lambda g: (path_sb[n][:, g, :].bitcast(FP4X4), plane[:, g, cols(n_in)]))
+            hits[i] = product(m, lambda g: (path_sb[n][:, g, :].bitcast(FP4X4), path_sc[n][:, g, :]))
 
         def value_product(i):
             n, m = divmod(i, M_TILES)
             value[i] = product(m, lambda g: (leaf_sb[n][:, g, :].bitcast(FP8X4), leaf_sc[4 * g :, cols(n)]))
 
-        def extra_product(i):
+        def extra_product(i, c0, c1):
             n, m = divmod(i, M_TILES)
+            first = n * PASSES
             extra[i] = product(
-                m, lambda g: (corr_codes[n * PASSES + g][:].bitcast(FP8X4), corr_scales[n * PASSES + g][:])
+                m,
+                lambda g: (corr_codes[first + g][:, c0:c1].bitcast(FP8X4), corr_scales[first + g][:, c0:c1]),
+                c1 - c0,
             )
 
         def interleave_views(c, c0, c1):
@@ -241,7 +261,7 @@ def tile_tree_path_leaf_response_s10_kernel(
             return dst, src
 
         def interleave_scalar(c):
-            corr_bf[c] = stage.tile([P, N_TILE * PACK], BF16, name="corr_bf", align_bytes=64, bufs=3)
+            corr_bf[c] = stage.tile([P, N_TILE * PACK], BF16, name="corr_bf", align_bytes=64, bufs=4)
             dst, src = interleave_views(c, 0, SCALAR_COLS)
             nc.scalar.copy(out=dst, in_=src)
 
@@ -256,19 +276,22 @@ def tile_tree_path_leaf_response_s10_kernel(
 
         def subtract_count(i):
             reach[i] = stage.tile([P, N_TILE], F32, name="reach", bufs=4)
-            nc.vector.tensor_tensor(out=reach[i][:], in0=hits[i][:], in1=count_all[:, cols(i // M_TILES)], op=ALU.subtract)
+            nc.vector.tensor_tensor(out=reach[i][:], in0=hits[i], in1=count_all[:, cols(i // M_TILES)], op=ALU.subtract)
 
         def sigmoid(i):
-            nc.scalar.activation(out=reach[i][:], in_=reach[i][:], func=ACT.Sigmoid)
+            nc.scalar.activation(out=reach[i][:], in_=reach[i][:], func=ACT.Tanh, scale=0.5)
 
         def gate_value(i):
             result[i] = keep.tile([P, N_TILE], F32, name="result%d" % i)
-            nc.vector.tensor_tensor(out=result[i][:], in0=value[i][:], in1=reach[i][:], op=ALU.mult)
+            nc.vector.scalar_tensor_tensor(
+                out=result[i][:], in0=reach[i][:], scalar=1.0, in1=value[i], op0=ALU.add, op1=ALU.mult
+            )
 
-        def add_extra(i):
+        def add_extra(i, c0, c1):
             n, m = divmod(i, M_TILES)
-            nc.vector.tensor_tensor(out=result[i][:], in0=extra[i][:], in1=result[i][:], op=ALU.add)
-            nc.sync.dma_start(out=out[m * P : (m + 1) * P, cols(n)], in_=result[i][:])
+            part = result[i][:, c0:c1]
+            nc.vector.scalar_tensor_tensor(out=part, in0=part, scalar=0.5, in1=extra[i], op0=ALU.mult, op1=ALU.add)
+            nc.sync.dma_start(out=out[m * P : (m + 1) * P, n * N_TILE + c0 : n * N_TILE + c1], in_=part)
 
         compare(0, 0)
         for m in range(M_TILES):
@@ -278,42 +301,48 @@ def tile_tree_path_leaf_response_s10_kernel(
             quantize_d(m, 0)
             if m + 1 < M_TILES:
                 compare(m + 1, 0)
-                quantize_d(m, 1)
+            quantize_d(m, 1)
 
-        hits_product(0)
-        hits_product(1)
-        value_product(0)
-        value_product(1)
-        hits_product(2)
-        value_product(2)
-        interleave_scalar(0)
+        def gated_groups(tiles):
+            order = [("hits", tiles[0])]
+            for i in tiles:
+                if i + 1 in tiles:
+                    order.append(("hits", i + 1))
+                order.append(("value", i))
+            return order
 
-        for i in range(TILES):
-            if i >= M_TILES - 1:
-                hits_product(i)
-                value_product(i)
-            subtract_count(i)
-            if i == 0:
-                quantize_d(M_TILES - 1, 1)
-            if i >= 3:
-                interleave_vector(i - 3)
-            if i >= 1:
-                gate_value(i - 1)
-            if i >= 3:
-                quantize_corr(i - 3)
-            sigmoid(i)
-            if i >= 2:
-                interleave_scalar(i - 1)
+        def extra_groups(tiles):
+            return [("extra", i, 0, N_TILE) for i in tiles]
+
         last = TILES - 1
-        for i in range(TILES):
-            extra_product(i)
-            late = CHUNKS - 3 + i // 2
-            if i % 2 == 1 and late < CHUNKS:
-                interleave_vector(late)
-            add_extra(i)
-            if i == 1:
-                gate_value(last)
-            if i % 2 == 1 and late < CHUNKS:
-                quantize_corr(late)
-            if i == 1:
-                interleave_scalar(CHUNKS - 1)
+        order = (
+            gated_groups(range(0, 2 * M_TILES))
+            + extra_groups(range(0, M_TILES))
+            + gated_groups(range(2 * M_TILES, TILES))
+            + extra_groups(range(M_TILES, last))
+            + [("extra", last, 0, N_TILE // 2), ("extra", last, N_TILE // 2, N_TILE)]
+        )
+
+        interleave_scalar(0)
+        for j, group in enumerate(order):
+            kind, i = group[:2]
+            ready = (j - 2 - QUANT_LAG) // 2 if j % 2 == 0 else -1
+            if kind == "hits":
+                hits_product(i)
+            elif kind == "value":
+                value_product(i)
+            else:
+                extra_product(*group[1:])
+            if 0 <= ready < CHUNKS:
+                interleave_vector(ready)
+            if kind == "hits":
+                subtract_count(i)
+                sigmoid(i)
+            if j >= GATE_LAG and order[j - GATE_LAG][0] == "value":
+                gate_value(order[j - GATE_LAG][1])
+            if kind == "extra":
+                add_extra(*group[1:])
+            if 0 <= ready < CHUNKS:
+                quantize_corr(ready)
+            if j % 2 == 0 and 1 <= (j - 2) // 2 < CHUNKS:
+                interleave_scalar((j - 2) // 2)

@@ -26,9 +26,10 @@ N_TILES = N // N_TILE
 TILES = M_TILES * N_TILES
 CHUNKS = N_TILES * PASSES
 BANKS = 8
+ALIGN = 64
 SCALAR_COLS = 416
 GATE_LAG = 4
-QUANT_LAG = 6
+QUANT_LAG = 5
 THR_ROW, GAIN_ROW, COUNT_ROW = 0, PASSES, 2 * PASSES
 VEC_ROWS = COUNT_ROW + N_TILES
 
@@ -60,8 +61,8 @@ def tile_tree_path_leaf_response_s10_kernel(
 
         path_sc = {}
         for n in range(N_TILES):
-            path_sc[n] = keep.tile([P, PASSES, N_TILE], U8, name="path_sc%d" % n, align_bytes=64)
-        leaf_sc = keep.tile([P, N], U8, name="leaf_sc", align_bytes=64)
+            path_sc[n] = keep.tile([P, PASSES, N_TILE], U8, name="path_sc%d" % n, align_bytes=ALIGN)
+        leaf_sc = keep.tile([P, N], U8, name="leaf_sc", align_bytes=ALIGN)
         nc.vector.memset(leaf_sc[:].bitcast(I32), 0)
         for n in range(N_TILES):
             nc.vector.memset(path_sc[n][:].rearrange("p g n -> p (g n)").bitcast(I32), 0)
@@ -77,20 +78,24 @@ def tile_tree_path_leaf_response_s10_kernel(
             for h in range(h0, h1):
                 x_sb[m, h] = t[:, (h - h0) * 2 * K_PASS : (h - h0 + 1) * 2 * K_PASS]
 
-        def load_path(n):
-            t = keep.tile([P, PASSES, 2 * N_TILE], U8, name="path%d" % n, align_bytes=64)
-            src = path_words[:, :, n * 2 * N_TILE : (n + 1) * 2 * N_TILE].rearrange("g p b -> p g b")
-            nc.sync.dma_start(out=t[:].bitcast(I32), in_=src.bitcast(I32))
-            path_sb[n] = t
+        def load_path_scales(n):
             for q in range(4):
                 rows = path_scales[:, 4 * q : 4 * q + 4, n * N_TILE : (n + 1) * N_TILE].rearrange("g r n -> r g n")
                 nc.sync.dma_start(out=path_sc[n][32 * q : 32 * q + 4, :, :].bitcast(I32), in_=rows.bitcast(I32))
 
-        def load_leaf(n):
-            t = keep.tile([P, PASSES, N_TILE], U32, name="leaf%d" % n, align_bytes=64)
-            src = leaf_words.rearrange("g p n t -> p g (n t)")[:, :, n * 4 * N_TILE : (n + 1) * 4 * N_TILE]
+        def load_path(n, g0=0, g1=PASSES):
+            t = keep.tile([P, g1 - g0, 2 * N_TILE], U8, name="path%d_%d" % (n, g0), align_bytes=ALIGN)
+            src = path_words[g0:g1, :, n * 2 * N_TILE : (n + 1) * 2 * N_TILE].rearrange("g p b -> p g b")
             nc.sync.dma_start(out=t[:].bitcast(I32), in_=src.bitcast(I32))
-            leaf_sb[n] = t
+            for g in range(g0, g1):
+                path_sb[n, g] = t[:, g - g0, :]
+
+        def load_leaf(n, g0=0, g1=PASSES):
+            t = keep.tile([P, g1 - g0, N_TILE], U32, name="leaf%d_%d" % (n, g0), align_bytes=ALIGN)
+            src = leaf_words.rearrange("g p n t -> p g (n t)")[:, g0:g1, n * 4 * N_TILE : (n + 1) * 4 * N_TILE]
+            nc.sync.dma_start(out=t[:].bitcast(I32), in_=src.bitcast(I32))
+            for g in range(g0, g1):
+                leaf_sb[n, g] = t[:, g - g0, :]
 
         def load_leaf_scales():
             for q in range(4):
@@ -111,16 +116,21 @@ def tile_tree_path_leaf_response_s10_kernel(
         load_x(0, 1, 2)
         for m in range(1, M_TILES):
             load_x(m, 0, 2)
-        load_path(0)
-        load_leaf(0)
+        load_path_scales(0)
+        load_path(0, 0, 2)
+        load_path(0, 2, PASSES)
+        load_leaf(0, 0, 2)
         load_leaf_scales()
+        load_leaf(0, 2, PASSES)
         load_corr(0)
         load_path(1)
+        load_path_scales(1)
         load_corr(1)
         load_leaf(1)
         for c in range(2, 7):
             load_corr(c)
         load_path(2)
+        load_path_scales(2)
         load_leaf(2)
         for c in range(7, CHUNKS):
             load_corr(c)
@@ -168,8 +178,8 @@ def tile_tree_path_leaf_response_s10_kernel(
                         func=ACT.Copy,
                     )
 
-        transpose_x(0, 0)
         transpose_vectors()
+        transpose_x(0, 0)
         transpose_x(0, 1)
         spread_count()
         for m in range(1, M_TILES):
@@ -181,7 +191,7 @@ def tile_tree_path_leaf_response_s10_kernel(
         d_scales = {}
 
         def compare(m, h):
-            t = stage.tile([P, 2 * K_PASS], BF16, name="d_bf", align_bytes=64, bufs=4)
+            t = stage.tile([P, 2 * K_PASS], BF16, name="d_bf", align_bytes=ALIGN, bufs=4)
             shape = [P, 2, P, 2, 2]
             nc.vector.tensor_tensor(
                 out=t[:].rearrange("p (g m u e) -> p g m u e", g=2, u=2, e=2),
@@ -201,8 +211,8 @@ def tile_tree_path_leaf_response_s10_kernel(
             )
 
         def quantize_d(m, h):
-            codes = keep.tile([P, 2 * P], U32, name="d_codes%d_%d" % (m, h), align_bytes=64)
-            scales = keep.tile([P, 2 * P], U8, name="d_scales%d_%d" % (m, h), align_bytes=64)
+            codes = keep.tile([P, 2 * P], U32, name="d_codes%d_%d" % (m, h), align_bytes=ALIGN)
+            scales = keep.tile([P, 2 * P], U8, name="d_scales%d_%d" % (m, h), align_bytes=ALIGN)
             nc.vector.quantize_mx(out=codes[:].bitcast(FP8X4), scales=scales[:], in_=d_bf[m, h][:])
             for gg in range(2):
                 d_codes[m, 2 * h + gg] = codes[:, gg * P : (gg + 1) * P]
@@ -240,11 +250,11 @@ def tile_tree_path_leaf_response_s10_kernel(
 
         def hits_product(i):
             n, m = divmod(i, M_TILES)
-            hits[i] = product(m, lambda g: (path_sb[n][:, g, :].bitcast(FP4X4), path_sc[n][:, g, :]))
+            hits[i] = product(m, lambda g: (path_sb[n, g].bitcast(FP4X4), path_sc[n][:, g, :]))
 
         def value_product(i):
             n, m = divmod(i, M_TILES)
-            value[i] = product(m, lambda g: (leaf_sb[n][:, g, :].bitcast(FP8X4), leaf_sc[4 * g :, cols(n)]))
+            value[i] = product(m, lambda g: (leaf_sb[n, g].bitcast(FP8X4), leaf_sc[4 * g :, cols(n)]))
 
         def extra_product(i, c0, c1):
             n, m = divmod(i, M_TILES)
@@ -261,7 +271,7 @@ def tile_tree_path_leaf_response_s10_kernel(
             return dst, src
 
         def interleave_scalar(c):
-            corr_bf[c] = stage.tile([P, N_TILE * PACK], BF16, name="corr_bf", align_bytes=64, bufs=4)
+            corr_bf[c] = stage.tile([P, N_TILE * PACK], BF16, name="corr_bf", align_bytes=ALIGN, bufs=4)
             dst, src = interleave_views(c, 0, SCALAR_COLS)
             nc.scalar.copy(out=dst, in_=src)
 
@@ -270,8 +280,8 @@ def tile_tree_path_leaf_response_s10_kernel(
             nc.vector.tensor_copy(out=dst, in_=src)
 
         def quantize_corr(c):
-            corr_codes[c] = keep.tile([P, N_TILE], U32, name="corr_codes%d" % c, align_bytes=64)
-            corr_scales[c] = keep.tile([P, N_TILE], U8, name="corr_scales%d" % c, align_bytes=64)
+            corr_codes[c] = keep.tile([P, N_TILE], U32, name="corr_codes%d" % c, align_bytes=ALIGN)
+            corr_scales[c] = keep.tile([P, N_TILE], U8, name="corr_scales%d" % c, align_bytes=ALIGN)
             nc.vector.quantize_mx(out=corr_codes[c][:].bitcast(FP8X4), scales=corr_scales[c][:], in_=corr_bf[c][:])
 
         def subtract_count(i):
@@ -304,11 +314,9 @@ def tile_tree_path_leaf_response_s10_kernel(
             quantize_d(m, 1)
 
         def gated_groups(tiles):
-            order = [("hits", tiles[0])]
+            order = []
             for i in tiles:
-                if i + 1 in tiles:
-                    order.append(("hits", i + 1))
-                order.append(("value", i))
+                order.extend([("hits", i), ("value", i)])
             return order
 
         def extra_groups(tiles):
@@ -316,7 +324,8 @@ def tile_tree_path_leaf_response_s10_kernel(
 
         last = TILES - 1
         order = (
-            gated_groups(range(0, 2 * M_TILES))
+            [("hits", 0), ("hits", 1), ("value", 0), ("value", 1)]
+            + gated_groups(range(2, 2 * M_TILES))
             + extra_groups(range(0, M_TILES))
             + gated_groups(range(2 * M_TILES, TILES))
             + extra_groups(range(M_TILES, last))
@@ -326,7 +335,7 @@ def tile_tree_path_leaf_response_s10_kernel(
         interleave_scalar(0)
         for j, group in enumerate(order):
             kind, i = group[:2]
-            ready = (j - 2 - QUANT_LAG) // 2 if j % 2 == 0 else -1
+            ready = (j - 2 - QUANT_LAG) // 2 if (j - QUANT_LAG) % 2 == 0 else -1
             if kind == "hits":
                 hits_product(i)
             elif kind == "value":

@@ -26,7 +26,7 @@ N_TILES = N // N_TILE
 TILES = M_TILES * N_TILES
 CHUNKS = N_TILES * PASSES
 BANKS = 8
-ALIGN = 64
+ALIGN = 256
 SCALAR_COLS = 416
 GATE_LAG = 4
 QUANT_LAG = 5
@@ -303,15 +303,10 @@ def tile_tree_path_leaf_response_s10_kernel(
             nc.vector.scalar_tensor_tensor(out=part, in0=part, scalar=0.5, in1=extra[i], op0=ALU.mult, op1=ALU.add)
             nc.sync.dma_start(out=out[m * P : (m + 1) * P, n * N_TILE + c0 : n * N_TILE + c1], in_=part)
 
-        compare(0, 0)
         for m in range(M_TILES):
-            compare(m, 1)
-            weight(m, 0)
-            weight(m, 1)
-            quantize_d(m, 0)
-            if m + 1 < M_TILES:
-                compare(m + 1, 0)
-            quantize_d(m, 1)
+            for step in (compare, weight, quantize_d):
+                step(m, 0)
+                step(m, 1)
 
         def gated_groups(tiles):
             order = []

from contextlib import ExitStack

import concourse.mybir as mybir
from concourse.masks import make_identity

M, K, N = 512, 2048, 1536
FLOPS = 3 * 2 * M * K * N

F32 = mybir.dt.float32
BF16 = mybir.dt.bfloat16
I32 = mybir.dt.int32
U32 = mybir.dt.uint32
U8 = mybir.dt.uint8
FP8X4 = mybir.dt.float8_e4m3fn_x4
FP4X4 = mybir.dt.float4_e2m1fn_x4
ALU = mybir.AluOpType
ACT = mybir.ActivationFunctionType

P = 128
PACK = 4
K_PASS = P * PACK
PASSES = K // K_PASS
N_TILE = 512
M_TILES = M // P
N_TILES = N // N_TILE
TILES = M_TILES * N_TILES
CHUNKS = N_TILES * PASSES
BANKS = 8
ALIGN = 256
SCALAR_COLS = 416
GATE_LAG = 4
QUANT_LAG = 5
THR_ROW, GAIN_ROW, COUNT_ROW = 0, PASSES, 2 * PASSES
VEC_ROWS = COUNT_ROW + N_TILES


def tile_tree_path_leaf_response_s10_kernel(
    tc, x, thr, gain, path_words, path_scales, count, leaf_words, leaf_scales, corr, out
):
    nc = tc.nc
    with ExitStack() as ctx:
        keep = ctx.enter_context(tc.tile_pool(name="keep", bufs=1))
        stage = ctx.enter_context(tc.tile_pool(name="stage", bufs=3))
        psum = ctx.enter_context(tc.psum_pool(name="psum", bufs=1))
        ctx.enter_context(tc.manual_schedule())

        def bank_tile(b):
            return psum.tile([P, N_TILE], F32, name="bank%d" % b)

        vec_rows = keep.tile([P, K_PASS], BF16, name="vec_rows")
        nc.gpsimd.memset(vec_rows[:].bitcast(I32), 0)
        ident = keep.tile([P, P], F32, name="ident")
        make_identity(nc, ident[:])

        def load_vectors():
            count_rows = count.rearrange("(r k) -> r k", k=K_PASS)
            nc.sync.dma_start(out=vec_rows[THR_ROW:GAIN_ROW, :], in_=thr.rearrange("(r k) -> r k", k=K_PASS))
            nc.sync.dma_start(out=vec_rows[GAIN_ROW:COUNT_ROW, :], in_=gain.rearrange("(r k) -> r k", k=K_PASS))
            nc.sync.dma_start(out=vec_rows[COUNT_ROW : COUNT_ROW + 2, :], in_=count_rows[:2, :])
            nc.sync.dma_start(out=vec_rows[COUNT_ROW + 2 : VEC_ROWS, :], in_=count_rows[2:, :])

        path_sc = {}
        for n in range(N_TILES):
            path_sc[n] = keep.tile([P, PASSES, N_TILE], U8, name="path_sc%d" % n, align_bytes=ALIGN)
        leaf_sc = keep.tile([P, N], U8, name="leaf_sc", align_bytes=ALIGN)
        nc.vector.memset(leaf_sc[:].bitcast(I32), 0)
        for n in range(N_TILES):
            nc.vector.memset(path_sc[n][:].rearrange("p g n -> p (g n)").bitcast(I32), 0)

        x_sb = {}
        path_sb = {}
        leaf_sb = {}
        corr_sb = {}

        def load_x(m, h0, h1):
            t = keep.tile([P, (h1 - h0) * 2 * K_PASS], BF16, name="x%d_%d" % (m, h0))
            nc.sync.dma_start(out=t[:], in_=x[m * P : (m + 1) * P, h0 * 2 * K_PASS : h1 * 2 * K_PASS])
            for h in range(h0, h1):
                x_sb[m, h] = t[:, (h - h0) * 2 * K_PASS : (h - h0 + 1) * 2 * K_PASS]

        def load_path_scales(n):
            for q in range(4):
                rows = path_scales[:, 4 * q : 4 * q + 4, n * N_TILE : (n + 1) * N_TILE].rearrange("g r n -> r g n")
                nc.sync.dma_start(out=path_sc[n][32 * q : 32 * q + 4, :, :].bitcast(I32), in_=rows.bitcast(I32))

        def load_path(n, g0=0, g1=PASSES):
            t = keep.tile([P, g1 - g0, 2 * N_TILE], U8, name="path%d_%d" % (n, g0), align_bytes=ALIGN)
            src = path_words[g0:g1, :, n * 2 * N_TILE : (n + 1) * 2 * N_TILE].rearrange("g p b -> p g b")
            nc.sync.dma_start(out=t[:].bitcast(I32), in_=src.bitcast(I32))
            for g in range(g0, g1):
                path_sb[n, g] = t[:, g - g0, :]

        def load_leaf(n, g0=0, g1=PASSES):
            t = keep.tile([P, g1 - g0, N_TILE], U32, name="leaf%d_%d" % (n, g0), align_bytes=ALIGN)
            src = leaf_words.rearrange("g p n t -> p g (n t)")[:, g0:g1, n * 4 * N_TILE : (n + 1) * 4 * N_TILE]
            nc.sync.dma_start(out=t[:].bitcast(I32), in_=src.bitcast(I32))
            for g in range(g0, g1):
                leaf_sb[n, g] = t[:, g - g0, :]

        def load_leaf_scales():
            for q in range(4):
                nc.sync.dma_start(
                    out=leaf_sc[32 * q : 32 * q + 16, :].bitcast(I32),
                    in_=leaf_scales[:, 4 * q : 4 * q + 4, :].bitcast(I32),
                )

        def load_corr(c):
            n, g = divmod(c, PASSES)
            t = keep.tile([P, PACK, N_TILE], BF16, name="corr%d" % c)
            src = corr[g * K_PASS : (g + 1) * K_PASS, n * N_TILE : (n + 1) * N_TILE]
            nc.sync.dma_start(out=t[:], in_=src.rearrange("(p t) n -> p t n", t=PACK))
            corr_sb[c] = t

        load_x(0, 0, 1)
        load_vectors()
        load_x(0, 1, 2)
        for m in range(1, M_TILES):
            load_x(m, 0, 2)
        load_path_scales(0)
        load_path(0, 0, 2)
        load_path(0, 2, PASSES)
        load_leaf(0, 0, 2)
        load_leaf_scales()
        load_leaf(0, 2, PASSES)
        load_corr(0)
        load_path(1)
        load_path_scales(1)
        load_corr(1)
        load_leaf(1)
        for c in range(2, 7):
            load_corr(c)
        load_path(2)
        load_path_scales(2)
        load_leaf(2)
        for c in range(7, CHUNKS):
            load_corr(c)

        xt = {}

        def transpose_x(m, h):
            bank = bank_tile(2 * m + h)
            words = x_sb[m, h].bitcast(F32)
            for gg in range(2):
                for u in range(2):
                    col = (2 * u + gg) * P
                    nc.tensor.transpose(
                        bank[:, col : col + P], words[:, 256 * gg + u : 256 * (gg + 1) : 2], ident[:]
                    )
            xt[m, h] = bank

        count_all = keep.tile([P, N], BF16, name="count_all")

        vec_cols = keep.tile([P, VEC_ROWS, 2], F32, name="vec_cols")
        vec_bf = vec_cols[:].bitcast(BF16)

        def transpose_vectors():
            bank = bank_tile(BANKS - 3)
            words = vec_rows[:].bitcast(F32)
            for u in range(2):
                nc.tensor.transpose(bank[:, u * P : (u + 1) * P], words[:, u::2], ident[:])
            src = bank[:, : 2 * P].rearrange("p (u r) -> p r u", u=2)
            nc.vector.tensor_copy(out=vec_cols[:], in_=src[:, :VEC_ROWS, :])

        def spread_count():
            for n0 in range(0, N_TILES, 2):
                bank = bank_tile(BANKS - 2 + n0 // 2)
                tiles = range(n0, min(n0 + 2, N_TILES))
                for n in tiles:
                    for u in range(2):
                        col = (2 * (n - n0) + u) * P
                        column = vec_cols[:, COUNT_ROW + n, u : u + 1]
                        nc.tensor.transpose(bank[:, col : col + P], column.to_broadcast([P, P]), ident[:])
                for n in tiles:
                    pairs = bank[:, (n - n0) * 2 * P : (n - n0 + 1) * 2 * P].bitcast(BF16)
                    nc.scalar.activation(
                        out=count_all[:, n * N_TILE : (n + 1) * N_TILE].rearrange("q (p u e) -> q p u e", u=2, e=2),
                        in_=pairs.rearrange("q (u p e) -> q p u e", u=2, e=2),
                        func=ACT.Copy,
                    )

        transpose_vectors()
        transpose_x(0, 0)
        transpose_x(0, 1)
        spread_count()
        for m in range(1, M_TILES):
            transpose_x(m, 0)
            transpose_x(m, 1)

        d_bf = {}
        d_codes = {}
        d_scales = {}

        def compare(m, h):
            t = stage.tile([P, 2 * K_PASS], BF16, name="d_bf", align_bytes=ALIGN, bufs=4)
            shape = [P, 2, P, 2, 2]
            nc.vector.tensor_tensor(
                out=t[:].rearrange("p (g m u e) -> p g m u e", g=2, u=2, e=2),
                in0=xt[m, h][:].bitcast(BF16).rearrange("p (u g m e) -> p g m u e", u=2, g=2, e=2),
                in1=vec_bf[:, THR_ROW + 2 * h : THR_ROW + 2 * h + 2, :].rearrange("p g (u e) -> p g u e", e=2).unsqueeze(2).to_broadcast(shape),
                op=ALU.is_gt,
            )
            d_bf[m, h] = t

        def weight(m, h):
            view = d_bf[m, h][:].rearrange("p (g m t) -> p g m t", g=2, t=PACK)
            nc.vector.tensor_tensor(
                out=view,
                in0=view,
                in1=vec_bf[:, GAIN_ROW + 2 * h : GAIN_ROW + 2 * h + 2, :].unsqueeze(2).to_broadcast([P, 2, P, PACK]),
                op=ALU.mult,
            )

        def quantize_d(m, h):
            codes = keep.tile([P, 2 * P], U32, name="d_codes%d_%d" % (m, h), align_bytes=ALIGN)
            scales = keep.tile([P, 2 * P], U8, name="d_scales%d_%d" % (m, h), align_bytes=ALIGN)
            nc.vector.quantize_mx(out=codes[:].bitcast(FP8X4), scales=scales[:], in_=d_bf[m, h][:])
            for gg in range(2):
                d_codes[m, 2 * h + gg] = codes[:, gg * P : (gg + 1) * P]
                d_scales[m, 2 * h + gg] = scales[:, gg * P : (gg + 1) * P]

        groups = []

        def product(m, rhs_of_pass, width=N_TILE):
            bank = bank_tile(len(groups) % BANKS)
            groups.append(bank)
            for g in range(PASSES):
                rhs, rhs_scale = rhs_of_pass(g)
                nc.tensor.matmul_mx(
                    out=bank[:, :width],
                    lhsT=d_codes[m, g].bitcast(FP8X4),
                    lhsT_scale=d_scales[m, g],
                    rhs=rhs,
                    rhs_scale=rhs_scale,
                    start=(g == 0),
                    stop=(g == PASSES - 1),
                )
            return bank[:, :width]

        hits = {}
        value = {}
        extra = {}
        corr_bf = {}
        corr_codes = {}
        corr_scales = {}
        reach = {}
        result = {}

        def cols(n):
            return slice(n * N_TILE, (n + 1) * N_TILE)

        def hits_product(i):
            n, m = divmod(i, M_TILES)
            hits[i] = product(m, lambda g: (path_sb[n, g].bitcast(FP4X4), path_sc[n][:, g, :]))

        def value_product(i):
            n, m = divmod(i, M_TILES)
            value[i] = product(m, lambda g: (leaf_sb[n, g].bitcast(FP8X4), leaf_sc[4 * g :, cols(n)]))

        def extra_product(i, c0, c1):
            n, m = divmod(i, M_TILES)
            first = n * PASSES
            extra[i] = product(
                m,
                lambda g: (corr_codes[first + g][:, c0:c1].bitcast(FP8X4), corr_scales[first + g][:, c0:c1]),
                c1 - c0,
            )

        def interleave_views(c, c0, c1):
            dst = corr_bf[c][:, c0 * PACK : c1 * PACK].rearrange("p (c i t) -> p c t i", i=4, t=PACK)
            src = corr_sb[c][:, :, c0:c1].rearrange("p t (c i) -> p c t i", i=4)
            return dst, src

        def interleave_scalar(c):
            corr_bf[c] = stage.tile([P, N_TILE * PACK], BF16, name="corr_bf", align_bytes=ALIGN, bufs=4)
            dst, src = interleave_views(c, 0, SCALAR_COLS)
            nc.scalar.copy(out=dst, in_=src)

        def interleave_vector(c):
            dst, src = interleave_views(c, SCALAR_COLS, N_TILE)
            nc.vector.tensor_copy(out=dst, in_=src)

        def quantize_corr(c):
            corr_codes[c] = keep.tile([P, N_TILE], U32, name="corr_codes%d" % c, align_bytes=ALIGN)
            corr_scales[c] = keep.tile([P, N_TILE], U8, name="corr_scales%d" % c, align_bytes=ALIGN)
            nc.vector.quantize_mx(out=corr_codes[c][:].bitcast(FP8X4), scales=corr_scales[c][:], in_=corr_bf[c][:])

        def subtract_count(i):
            reach[i] = stage.tile([P, N_TILE], F32, name="reach", bufs=4)
            nc.vector.tensor_tensor(out=reach[i][:], in0=hits[i], in1=count_all[:, cols(i // M_TILES)], op=ALU.subtract)

        def sigmoid(i):
            nc.scalar.activation(out=reach[i][:], in_=reach[i][:], func=ACT.Tanh, scale=0.5)

        def gate_value(i):
            result[i] = keep.tile([P, N_TILE], F32, name="result%d" % i)
            nc.vector.scalar_tensor_tensor(
                out=result[i][:], in0=reach[i][:], scalar=1.0, in1=value[i], op0=ALU.add, op1=ALU.mult
            )

        def add_extra(i, c0, c1):
            n, m = divmod(i, M_TILES)
            part = result[i][:, c0:c1]
            nc.vector.scalar_tensor_tensor(out=part, in0=part, scalar=0.5, in1=extra[i], op0=ALU.mult, op1=ALU.add)
            nc.sync.dma_start(out=out[m * P : (m + 1) * P, n * N_TILE + c0 : n * N_TILE + c1], in_=part)

        for m in range(M_TILES):
            for step in (compare, weight, quantize_d):
                step(m, 0)
                step(m, 1)

        def gated_groups(tiles):
            order = []
            for i in tiles:
                order.extend([("hits", i), ("value", i)])
            return order

        def extra_groups(tiles):
            return [("extra", i, 0, N_TILE) for i in tiles]

        last = TILES - 1
        order = (
            [("hits", 0), ("hits", 1), ("value", 0), ("value", 1)]
            + gated_groups(range(2, 2 * M_TILES))
            + extra_groups(range(0, M_TILES))
            + gated_groups(range(2 * M_TILES, TILES))
            + extra_groups(range(M_TILES, last))
            + [("extra", last, 0, N_TILE // 2), ("extra", last, N_TILE // 2, N_TILE)]
        )

        interleave_scalar(0)
        for j, group in enumerate(order):
            kind, i = group[:2]
            ready = (j - 2 - QUANT_LAG) // 2 if (j - QUANT_LAG) % 2 == 0 else -1
            if kind == "hits":
                hits_product(i)
            elif kind == "value":
                value_product(i)
            else:
                extra_product(*group[1:])
            if 0 <= ready < CHUNKS:
                interleave_vector(ready)
            if kind == "hits":
                subtract_count(i)
                sigmoid(i)
            if j >= GATE_LAG and order[j - GATE_LAG][0] == "value":
                gate_value(order[j - GATE_LAG][1])
            if kind == "extra":
                add_extra(*group[1:])
            if 0 <= ready < CHUNKS:
                quantize_corr(ready)
            if j % 2 == 0 and 1 <= (j - 2) // 2 < CHUNKS:
                interleave_scalar((j - 2) // 2)
